import numpy as np
CORES = [2,3,6,7,58,59,62,63,114,115,118,119]
N = 12
TK = 256
EPS = 0.01
GRP = [[0,1,4,5,8,9,10],[2,3,6,7,11]]
def setup_inputs(rng):
    return {"x": rng.standard_normal((N, 128, TK), dtype=np.float32) * (0.5 + np.abs(rng.standard_normal((1, 1, TK), dtype=np.float32))) + rng.standard_normal((1, 1, TK), dtype=np.float32)}
def setup_inputs_big(rng):
    d = setup_inputs(rng)
    for k in ("x",): d[k] = (d[k].astype(np.float32) * 1024.0).astype(d[k].dtype)
    return d
def setup_inputs_small(rng):
    d = setup_inputs(rng)
    for k in ("x",): d[k] = (d[k].astype(np.float32) * (1 / 1024.0)).astype(d[k].dtype)
    return d
def setup_inputs_apart(rng):
    d = setup_inputs(rng)
    f = (10.0 ** rng.permutation(np.linspace(-1.5, 1.5, N))).astype(np.float32).reshape(N, 1, 1)
    for k in ("x",): d[k] = (d[k].astype(np.float32) * f).astype(d[k].dtype)
    return d
def setup_inputs_mixed(rng):
    d = setup_inputs(rng)
    f = (10.0 ** rng.uniform(-3, 3, (1, 1, TK))).astype(np.float32); shape = rng.integers(3, size=(1, 1, TK))
    for k in ("x",):
        x = d[k].astype(np.float32)
        m = x.mean(axis=(0, 1), keepdims=True); level = m + np.sign(x - m) * np.abs(x - m).mean(axis=(0, 1), keepdims=True) * rng.uniform(0.9, 1.1, x.shape).astype(np.float32)
        other = x * np.where(rng.random(x.shape) < 0.5, 0.1, 1.0).astype(np.float32)
        d[k] = (np.where(shape == 1, level, np.where(shape == 2, other, x)) * f).astype(d[k].dtype)
    return d
def setup_inputs_offset(rng):
    d = setup_inputs(rng)
    x = d["x"]; spread = x.std(axis=(0, 1), keepdims=True)
    d["x"] = (x + spread * rng.uniform(16, 48, (1, 1, TK)) * rng.choice([-1.0, 1.0], (1, 1, TK))).astype(np.float32)
    return d
def reference(x):
    X = x.astype(np.float64); y = np.zeros_like(X)
    for m in GRP:
        Z = X[m]; D = 128 * len(m)
        Z = Z - Z.sum(axis=(0, 1)) / D
        y[m] = Z / np.sqrt((Z ** 2).sum(axis=(0, 1)) / D + EPS)
    return {"y": y.astype(np.float32)}

@@ -1,0 +1,145 @@
+from concourse.bass import DstId, RemoteDMATransfer
+from concourse.mybir import AluOpType, AxisListType, ActivationFunctionType
+
+EPS = 0.01
+RMAX = 7
+
+SCRATCH = {
+    "xs": ("sbuf", [128, 256], "float32"),
+    "ident": ("sbuf", [128, 128], "float32"),
+    "ja": ("sbuf", [128, 128], "float32"),
+    "jb": ("sbuf", [128, 128], "float32"),
+    "jc": ("sbuf", [128, 128], "float32"),
+    "jd": ("sbuf", [128, 128], "float32"),
+    "jr": ("sbuf", [128, 32], "float32"),
+    "land": ("sbuf", [128, 4 * RMAX], "float32"),
+    "st": ("sbuf", [128, 16], "float32"),
+    "yt0": ("sbuf", [128, 128], "float32"),
+    "yt1": ("sbuf", [128, 128], "float32"),
+    "ys": ("sbuf", [128, 256], "float32"),
+    "xt0": ("psum", [128, 512], "float32"),
+    "xt1": ("psum", [128, 512], "float32"),
+    "yo0": ("psum", [128, 512], "float32"),
+    "yo1": ("psum", [128, 512], "float32"),
+    "yo2": ("psum", [128, 512], "float32"),
+}
+SEMAPHORES = ["ones", "idn", "arr", "sent", "tb0", "tb1", "tb2", "cp0", "cp1", "cp2", "so0", "so1"] + [
+    n + h for n in ("ld", "tp", "mn", "sq", "sm", "dv", "qq", "bb", "sd", "nm", "rc", "nr") for h in ("0", "1")]
+
+
+def _bits(m):
+    return bin(m).count("1")
+
+
+def _peers(T, topo, core):
+    rank = T.rank_of(core)
+    grp = [m for m in T.tables["GRP"] if rank in m][0]
+    peers = [T.cores[r] for r in grp if r != rank]
+
+    def near(d):
+        a, b = topo.chip(core), topo.chip(d)
+        if a == b:
+            return 2
+        return 1 if (topo.mates(a, b) or topo.same_plane(a, b)) else 0
+    peers.sort(key=near)
+    mask = topo.mask(core, peers[0])
+    for d in peers:
+        mask &= topo.mask(core, d)
+    return grp, peers, mask
+
+
+def rank_program(g, core, T, topo):
+    rank = T.rank_of(core)
+    if rank is None:
+        return
+    grp, peers, mask = _peers(T, topo, core)
+    R = len(grp)
+    D = 128 * R
+    c0 = 4 * grp.index(rank)
+    S = T.sem
+    A = ActivationFunctionType
+    add, mult = AluOpType.add, AluOpType.mult
+    V, SC, PE, SY = g.vector, g.scalar, g.tensor, g.sync
+    xt = [T.xt0, T.xt1]
+    yt = [T.yt0, T.yt1]
+    junk = [T.ja, T.jb, T.jc, T.jd]
+
+    def col(t, c):
+        return t[:, c:c + 1]
+
+    SY.dma_start(T.xs[:, 0:128], T.x[:, 0:128]).then_inc(S.ld0, 16)
+    SC.dma_start(T.xs[:, 128:256], T.x[:, 128:256]).then_inc(S.ld1, 16)
+    V.memset(T.ident[:], 1.0).then_inc(S.ones, 1)
+    g.wait_ge(S.ones, 1)
+    g.affine_select(T.ident[:], T.ident[:], [[-1, 128]], AluOpType.is_equal, 0.0, 0, 1).then_inc(S.idn, 1)
+
+    PE.wait_ge(S.idn, 1)
+    for h in (0, 1):
+        PE.wait_ge(S["ld%d" % h], 16)
+        PE.transpose(xt[h][:, 0:128], T.xs[:, 128 * h:128 * h + 128], T.ident[:]).then_inc(S["tp%d" % h], 1)
+    for h in (0, 1):
+        SC.wait_ge(S["tp%d" % h], 1)
+        SC.activation(junk[2 * h][:], xt[h][:, 0:128], A.Copy, scale=-1.0 / 128.0,
+                      accum_out=col(T.land, c0 + h)).then_inc(S["mn%d" % h], 1)
+        SC.wait_ge(S["mn%d" % h], 1)
+        SC.activation(junk[2 * h + 1][:], xt[h][:, 0:128], A.Square, bias=col(T.land, c0 + h), scale=1.0,
+                      accum_out=col(T.land, c0 + 2 + h)).then_inc(S["sq%d" % h], 1)
+
+    for n in ("mn0", "mn1", "sq0", "sq1"):
+        g.wait_ge(S[n], 1)
+    slot = T.land[:, c0:c0 + 4]
+    ids = []
+    for d in peers:
+        rid, pid, _se = topo.addr(d)
+        ids.append(DstId(rid=rid, pnc=pid))
+    g.remote_dma_fused([RemoteDMATransfer(dst_ids=ids, dma_engine_mask=mask, remote_sem=S.arr, srcs=[slot],
+                                          dsts=[slot for _d in peers], alu_op=0)], local_sem=S.sent)
+    expect = sum(_bits(_peers(T, topo, d)[2]) for d in peers)
+
+    SC.wait_ge(S.arr, expect)
+    for h in (0, 1):
+        means = T.land[:, h:4 * R:4]
+        SC.activation(T.jr[:, 16 * h:16 * h + R], means, A.Copy, scale=1.0,
+                      accum_out=col(T.st, h)).then_inc(S["sm%d" % h], 1)
+        SC.wait_ge(S["sm%d" % h], 1)
+        SC.activation(T.jr[:, 16 * h + 8:16 * h + 8 + R], means, A.Square, bias=col(T.st, h), scale=-float(R),
+                      accum_out=col(T.st, 2 + h)).then_inc(S["dv%d" % h], 1)
+        SC.wait_ge(S["dv%d" % h], 1)
+        SC.wait_ge(S["bb%d" % h], 1)
+        SC.activation(col(T.st, 8 + h), col(T.st, 2 + h), A.Sqrt, bias=col(T.st, 6 + h),
+                      scale=1.0 / float(R ** 3)).then_inc(S["sd%d" % h], 1)
+    for n in ("tp0", "tp1", "sq0", "sq1"):
+        V.wait_ge(S[n], 1)
+    V.wait_ge(S.arr, expect)
+    for h in (0, 1):
+        V.tensor_reduce(col(T.st, 4 + h), T.land[:, 2 + h:4 * R:4], AxisListType.X, add).then_inc(S["qq%d" % h], 1)
+        V.wait_ge(S["qq%d" % h], 1)
+        V.tensor_scalar(col(T.st, 6 + h), col(T.st, 4 + h), 1.0 / float(D), EPS, mult, add).then_inc(S["bb%d" % h], 1)
+    for h in (0, 1):
+        V.wait_ge(S["sm%d" % h], 1)
+        V.tensor_scalar(col(T.st, 12 + h), col(T.st, h), 1.0 / float(R), None, mult).then_inc(S["nm%d" % h], 1)
+        V.wait_ge(S["sd%d" % h], 1)
+        V.reciprocal(col(T.st, 10 + h), col(T.st, 8 + h)).then_inc(S["rc%d" % h], 1)
+        V.wait_ge(S["nm%d" % h], 1)
+        V.wait_ge(S["rc%d" % h], 1)
+        V.tensor_scalar(yt[h][:], xt[h][:, 0:128], col(T.st, 12 + h), col(T.st, 10 + h), add, mult).then_inc(
+            S["nr%d" % h], 1)
+    PE.wait_ge(S.nr0, 1)
+    PE.transpose(T.yo0[:, 0:128], T.yt0[:], T.ident[:]).then_inc(S.tb0, 1)
+    PE.wait_ge(S.nr1, 1)
+    PE.transpose(T.yo1[:, 0:64], T.yt1[0:64, :], T.ident[0:64, 0:64]).then_inc(S.tb1, 1)
+    PE.transpose(T.yo2[:, 0:64], T.yt1[64:128, :], T.ident[64:128, 64:128]).then_inc(S.tb2, 1)
+    V.wait_ge(S.tb0, 1)
+    V.tensor_copy(T.ys[:, 0:128], T.yo0[:, 0:128]).then_inc(S.cp0, 1)
+    V.wait_ge(S.tb1, 1)
+    V.tensor_copy(T.ys[:, 128:192], T.yo1[:, 0:64]).then_inc(S.cp1, 1)
+    SC.wait_ge(S.tb2, 1)
+    SC.activation(T.ys[:, 192:256], T.yo2[:, 0:64], A.Copy).then_inc(S.cp2, 1)
+    SY.wait_ge(S.cp0, 1)
+    SY.dma_start(T.y[:, 0:128], T.ys[:, 0:128]).then_inc(S.so0, 16)
+    SY.wait_ge(S.cp1, 1)
+    SY.wait_ge(S.cp2, 1)
+    SY.dma_start(T.y[:, 128:256], T.ys[:, 128:256]).then_inc(S.so1, 16)
+    SY.wait_ge(S.so0, 16)
+    SY.wait_ge(S.so1, 16)
+    g.wait_ge(S.sent, _bits(mask))

@@ -13,7 +13,9 @@ SCRATCH = {
     "jd": ("sbuf", [128, 128], "float32"),
     "jr": ("sbuf", [128, 32], "float32"),
     "land": ("sbuf", [128, 4 * RMAX], "float32"),
-    "st": ("sbuf", [128, 16], "float32"),
+    "st": ("sbuf", [128, 24], "float32"),
+    "xr0": ("sbuf", [128, 128], "float32"),
+    "xr1": ("sbuf", [128, 128], "float32"),
     "yt0": ("sbuf", [128, 128], "float32"),
     "yt1": ("sbuf", [128, 128], "float32"),
     "ys": ("sbuf", [128, 256], "float32"),
@@ -23,7 +25,8 @@ SCRATCH = {
     "yo1": ("psum", [128, 512], "float32"),
     "yo2": ("psum", [128, 512], "float32"),
 }
-SEMAPHORES = ["ones", "idn", "arr", "sent", "tb0", "tb1", "tb2", "cp0", "cp1", "cp2", "so0", "so1"] + [
+SEMAPHORES = ["ones", "idn", "arr", "sent", "tb0", "tb1", "tb2", "cp0", "cp1", "cp2", "so0", "so1", "so2",
+              "ow", "rw", "rr", "ra", "rb", "xs0", "xs1"] + [
     n + h for n in ("ld", "tp", "mn", "sq", "sm", "dv", "qq", "bb", "sd", "nm", "rc", "nr") for h in ("0", "1")]
 
 
@@ -61,6 +64,7 @@ def rank_program(g, core, T, topo):
     add, mult = AluOpType.add, AluOpType.mult
     V, SC, PE, SY = g.vector, g.scalar, g.tensor, g.sync
     xt = [T.xt0, T.xt1]
+    xr = [T.xr0, T.xr1]
     yt = [T.yt0, T.yt1]
     junk = [T.ja, T.jb, T.jc, T.jd]
 
@@ -96,6 +100,22 @@ def rank_program(g, core, T, topo):
                                           dsts=[slot for _d in peers], alu_op=0)], local_sem=S.sent)
     expect = sum(_bits(_peers(T, topo, d)[2]) for d in peers)
 
+    SC.wait_ge(S.sq0, 1)
+    SC.wait_ge(S.sq1, 1)
+    SC.activation(T.st[:, 14:16], T.land[:, c0 + 2:c0 + 4], A.Sqrt, bias=EPS, scale=1.0 / 128.0).then_inc(S.ow, 1)
+    for n in ("tp0", "tp1", "sq0", "sq1", "ow"):
+        V.wait_ge(S[n], 1)
+    V.reciprocal(T.st[:, 16:18], T.st[:, 14:16]).then_inc(S.rw, 1)
+    V.wait_ge(S.rw, 1)
+    V.tensor_tensor(T.st[:, 18:20], T.st[:, 16:18], T.st[:, 16:18], mult).then_inc(S.rr, 1)
+    for h in (0, 1):
+        V.tensor_scalar(xr[h][:], xt[h][:, 0:128], col(T.st, 16 + h), None, mult).then_inc(S["xs%d" % h], 1)
+    V.wait_ge(S.rr, 1)
+    V.tensor_scalar(T.st[:, 20:22], T.st[:, 18:20], 1.0 / float(D), None, mult).then_inc(S.ra, 1)
+    V.tensor_scalar(T.st[:, 22:24], T.st[:, 18:20], 1.0 / float(R ** 3), None, mult).then_inc(S.rb, 1)
+    V.wait_ge(S.ra, 1)
+    SC.wait_ge(S.rb, 1)
+
     SC.wait_ge(S.arr, expect)
     for h in (0, 1):
         means = T.land[:, h:4 * R:4]
@@ -107,22 +127,23 @@ def rank_program(g, core, T, topo):
         SC.wait_ge(S["dv%d" % h], 1)
         SC.wait_ge(S["bb%d" % h], 1)
         SC.activation(col(T.st, 8 + h), col(T.st, 2 + h), A.Sqrt, bias=col(T.st, 6 + h),
-                      scale=1.0 / float(R ** 3)).then_inc(S["sd%d" % h], 1)
-    for n in ("tp0", "tp1", "sq0", "sq1"):
-        V.wait_ge(S[n], 1)
+                      scale=col(T.st, 22 + h)).then_inc(S["sd%d" % h], 1)
     V.wait_ge(S.arr, expect)
     for h in (0, 1):
         V.tensor_reduce(col(T.st, 4 + h), T.land[:, 2 + h:4 * R:4], AxisListType.X, add).then_inc(S["qq%d" % h], 1)
         V.wait_ge(S["qq%d" % h], 1)
-        V.tensor_scalar(col(T.st, 6 + h), col(T.st, 4 + h), 1.0 / float(D), EPS, mult, add).then_inc(S["bb%d" % h], 1)
+        V.tensor_scalar(col(T.st, 6 + h), col(T.st, 4 + h), float(D) * EPS, col(T.st, 20 + h), add, mult).then_inc(
+            S["bb%d" % h], 1)
     for h in (0, 1):
         V.wait_ge(S["sm%d" % h], 1)
-        V.tensor_scalar(col(T.st, 12 + h), col(T.st, h), 1.0 / float(R), None, mult).then_inc(S["nm%d" % h], 1)
+        V.tensor_scalar(col(T.st, 12 + h), col(T.st, h), 1.0 / float(R), col(T.st, 16 + h), mult, mult).then_inc(
+            S["nm%d" % h], 1)
         V.wait_ge(S["sd%d" % h], 1)
         V.reciprocal(col(T.st, 10 + h), col(T.st, 8 + h)).then_inc(S["rc%d" % h], 1)
         V.wait_ge(S["nm%d" % h], 1)
         V.wait_ge(S["rc%d" % h], 1)
-        V.tensor_scalar(yt[h][:], xt[h][:, 0:128], col(T.st, 12 + h), col(T.st, 10 + h), add, mult).then_inc(
+        V.wait_ge(S["xs%d" % h], 1)
+        V.tensor_scalar(yt[h][:], xr[h][:], col(T.st, 12 + h), col(T.st, 10 + h), add, mult).then_inc(
             S["nr%d" % h], 1)
     PE.wait_ge(S.nr0, 1)
     PE.transpose(T.yo0[:, 0:128], T.yt0[:], T.ident[:]).then_inc(S.tb0, 1)
@@ -138,8 +159,10 @@ def rank_program(g, core, T, topo):
     SY.wait_ge(S.cp0, 1)
     SY.dma_start(T.y[:, 0:128], T.ys[:, 0:128]).then_inc(S.so0, 16)
     SY.wait_ge(S.cp1, 1)
+    SY.dma_start(T.y[:, 128:192], T.ys[:, 128:192]).then_inc(S.so1, 16)
     SY.wait_ge(S.cp2, 1)
-    SY.dma_start(T.y[:, 128:256], T.ys[:, 128:256]).then_inc(S.so1, 16)
+    SY.dma_start(T.y[:, 192:256], T.ys[:, 192:256]).then_inc(S.so2, 16)
     SY.wait_ge(S.so0, 16)
     SY.wait_ge(S.so1, 16)
+    SY.wait_ge(S.so2, 16)
     g.wait_ge(S.sent, _bits(mask))

@@ -7,10 +7,11 @@ RMAX = 7
 SCRATCH = {
     "xs": ("sbuf", [128, 256], "float32"),
     "ident": ("sbuf", [128, 128], "float32"),
+    "negc": ("sbuf", [128, 4], "float32"),
+    "mh": ("sbuf", [128, 4], "float32"),
     "ja": ("sbuf", [128, 128], "float32"),
     "jb": ("sbuf", [128, 128], "float32"),
     "jc": ("sbuf", [128, 128], "float32"),
-    "jd": ("sbuf", [128, 128], "float32"),
     "jr": ("sbuf", [128, 32], "float32"),
     "land": ("sbuf", [128, 4 * RMAX], "float32"),
     "st": ("sbuf", [128, 24], "float32"),
@@ -19,6 +20,7 @@ SCRATCH = {
     "yt0": ("sbuf", [128, 128], "float32"),
     "yt1": ("sbuf", [128, 128], "float32"),
     "ys": ("sbuf", [128, 256], "float32"),
+    "pm": ("psum", [128, 512], "float32"),
     "xt0": ("psum", [128, 512], "float32"),
     "xt1": ("psum", [128, 512], "float32"),
     "yo0": ("psum", [128, 512], "float32"),
@@ -26,8 +28,8 @@ SCRATCH = {
     "yo2": ("psum", [128, 512], "float32"),
 }
 SEMAPHORES = ["ones", "idn", "arr", "sent", "tb0", "tb1", "tb2", "cp0", "cp1", "cp2", "so0", "so1", "so2",
-              "ow", "rw", "rr", "ra", "rb", "xs0", "xs1"] + [
-    n + h for n in ("ld", "tp", "mn", "sq", "sm", "dv", "qq", "bb", "sd", "nm", "rc", "nr") for h in ("0", "1")]
+              "ow", "rw", "rr", "ra", "rb", "xs0", "xs1", "ng", "mm", "me", "ml", "mn1"] + [
+    n + h for n in ("ld", "tp", "sq", "sm", "dv", "qq", "bb", "sd", "nm", "rc", "nr") for h in ("0", "1")]
 
 
 def _bits(m):
@@ -66,39 +68,58 @@ def rank_program(g, core, T, topo):
     xt = [T.xt0, T.xt1]
     xr = [T.xr0, T.xr1]
     yt = [T.yt0, T.yt1]
-    junk = [T.ja, T.jb, T.jc, T.jd]
 
     def col(t, c):
         return t[:, c:c + 1]
 
     SY.dma_start(T.xs[:, 0:128], T.x[:, 0:128]).then_inc(S.ld0, 16)
     SC.dma_start(T.xs[:, 128:256], T.x[:, 128:256]).then_inc(S.ld1, 16)
+    V.memset(T.negc[:], -1.0 / 128.0).then_inc(S.ng, 1)
     V.memset(T.ident[:], 1.0).then_inc(S.ones, 1)
     g.wait_ge(S.ones, 1)
     g.affine_select(T.ident[:], T.ident[:], [[-1, 128]], AluOpType.is_equal, 0.0, 0, 1).then_inc(S.idn, 1)
 
+    PE.wait_ge(S.ng, 1)
+    PE.wait_ge(S.ld0, 16)
+    PE.matmul(T.pm[:, 0:1], T.xs[:, 0:128], T.negc[:, 0:1], True, True).then_inc(S.mm, 1)
     PE.wait_ge(S.idn, 1)
-    for h in (0, 1):
-        PE.wait_ge(S["ld%d" % h], 16)
-        PE.transpose(xt[h][:, 0:128], T.xs[:, 128 * h:128 * h + 128], T.ident[:]).then_inc(S["tp%d" % h], 1)
-    for h in (0, 1):
-        SC.wait_ge(S["tp%d" % h], 1)
-        SC.activation(junk[2 * h][:], xt[h][:, 0:128], A.Copy, scale=-1.0 / 128.0,
-                      accum_out=col(T.land, c0 + h)).then_inc(S["mn%d" % h], 1)
-        SC.wait_ge(S["mn%d" % h], 1)
-        SC.activation(junk[2 * h + 1][:], xt[h][:, 0:128], A.Square, bias=col(T.land, c0 + h), scale=1.0,
-                      accum_out=col(T.land, c0 + 2 + h)).then_inc(S["sq%d" % h], 1)
+    PE.transpose(T.xt0[:, 0:128], T.xs[:, 0:128], T.ident[:]).then_inc(S.tp0, 1)
+    PE.wait_ge(S.ld1, 16)
+    PE.transpose(T.xt1[:, 0:128], T.xs[:, 128:256], T.ident[:]).then_inc(S.tp1, 1)
+    V.wait_ge(S.mm, 1)
+    V.tensor_copy(T.mh[:, 0:1], T.pm[:, 0:1]).then_inc(S.me, 1)
+    V.tensor_copy(col(T.land, c0), T.pm[:, 0:1]).then_inc(S.ml, 1)
+    SC.wait_ge(S.tp0, 1)
+    SC.wait_ge(S.me, 1)
+    SC.activation(T.ja[:], T.xt0[:, 0:128], A.Square, bias=T.mh[:, 0:1], scale=1.0,
+                  accum_out=col(T.land, c0 + 2)).then_inc(S.sq0, 1)
+    SC.wait_ge(S.tp1, 1)
+    SC.activation(T.jb[:], T.xt1[:, 0:128], A.Copy, scale=-1.0 / 128.0,
+                  accum_out=col(T.land, c0 + 1)).then_inc(S.mn1, 1)
+    SC.wait_ge(S.mn1, 1)
+    SC.activation(T.jc[:], T.xt1[:, 0:128], A.Square, bias=col(T.land, c0 + 1), scale=1.0,
+                  accum_out=col(T.land, c0 + 3)).then_inc(S.sq1, 1)
 
-    for n in ("mn0", "mn1", "sq0", "sq1"):
+    def ident_of(d):
+        rid, pid, _se = topo.addr(d)
+        return DstId(rid=rid, pnc=pid)
+
+    near, far = peers[-1], peers[:-1]
+    g.wait_ge(S.me, 1)
+    g.remote_dma_fused([RemoteDMATransfer(dst_ids=[ident_of(near)], dma_engine_mask=mask, remote_sem=S.arr,
+                                          srcs=[T.mh[:, 0:1]], dsts=[col(T.land, c0)], alu_op=0)], local_sem=S.sent)
+    for n in ("ml", "mn1", "sq0", "sq1"):
         g.wait_ge(S[n], 1)
     slot = T.land[:, c0:c0 + 4]
-    ids = []
+    g.remote_dma_fused([RemoteDMATransfer(dst_ids=[ident_of(d) for d in far], dma_engine_mask=mask, remote_sem=S.arr,
+                                          srcs=[slot], dsts=[slot for _d in far], alu_op=0)], local_sem=S.sent)
+    rest = T.land[:, c0 + 1:c0 + 4]
+    g.remote_dma_fused([RemoteDMATransfer(dst_ids=[ident_of(near)], dma_engine_mask=mask, remote_sem=S.arr,
+                                          srcs=[rest], dsts=[rest], alu_op=0)], local_sem=S.sent)
+    expect = 0
     for d in peers:
-        rid, pid, _se = topo.addr(d)
-        ids.append(DstId(rid=rid, pnc=pid))
-    g.remote_dma_fused([RemoteDMATransfer(dst_ids=ids, dma_engine_mask=mask, remote_sem=S.arr, srcs=[slot],
-                                          dsts=[slot for _d in peers], alu_op=0)], local_sem=S.sent)
-    expect = sum(_bits(_peers(T, topo, d)[2]) for d in peers)
+        _g, dp, dm = _peers(T, topo, d)
+        expect += _bits(dm) * (2 if dp[-1] == core else 1)
 
     SC.wait_ge(S.sq0, 1)
     SC.wait_ge(S.sq1, 1)
@@ -116,6 +137,7 @@ def rank_program(g, core, T, topo):
     V.wait_ge(S.ra, 1)
     SC.wait_ge(S.rb, 1)
 
+    SC.wait_ge(S.ml, 1)
     SC.wait_ge(S.arr, expect)
     for h in (0, 1):
         means = T.land[:, h:4 * R:4]
@@ -165,4 +187,4 @@ def rank_program(g, core, T, topo):
     SY.wait_ge(S.so0, 16)
     SY.wait_ge(S.so1, 16)
     SY.wait_ge(S.so2, 16)
-    g.wait_ge(S.sent, _bits(mask))
+    g.wait_ge(S.sent, 3 * _bits(mask))

from concourse.bass import DstId, RemoteDMATransfer
from concourse.mybir import AluOpType, AxisListType, ActivationFunctionType

EPS = 0.01
RMAX = 7

SCRATCH = {
    "xs": ("sbuf", [128, 256], "float32"),
    "ident": ("sbuf", [128, 128], "float32"),
    "negc": ("sbuf", [128, 4], "float32"),
    "mh": ("sbuf", [128, 4], "float32"),
    "ja": ("sbuf", [128, 128], "float32"),
    "jb": ("sbuf", [128, 128], "float32"),
    "jc": ("sbuf", [128, 128], "float32"),
    "jr": ("sbuf", [128, 32], "float32"),
    "land": ("sbuf", [128, 4 * RMAX], "float32"),
    "st": ("sbuf", [128, 24], "float32"),
    "xr0": ("sbuf", [128, 128], "float32"),
    "xr1": ("sbuf", [128, 128], "float32"),
    "yt0": ("sbuf", [128, 128], "float32"),
    "yt1": ("sbuf", [128, 128], "float32"),
    "ys": ("sbuf", [128, 256], "float32"),
    "pm": ("psum", [128, 512], "float32"),
    "xt0": ("psum", [128, 512], "float32"),
    "xt1": ("psum", [128, 512], "float32"),
    "yo0": ("psum", [128, 512], "float32"),
    "yo1": ("psum", [128, 512], "float32"),
    "yo2": ("psum", [128, 512], "float32"),
}
SEMAPHORES = ["ones", "idn", "arr", "sent", "tb0", "tb1", "tb2", "cp0", "cp1", "cp2", "so0", "so1", "so2",
              "ow", "rw", "rr", "ra", "rb", "xs0", "xs1", "ng", "mm", "me", "ml", "mn1"] + [
    n + h for n in ("ld", "tp", "sq", "sm", "dv", "qq", "bb", "sd", "nm", "rc", "nr") for h in ("0", "1")]


def _bits(m):
    return bin(m).count("1")


def _peers(T, topo, core):
    rank = T.rank_of(core)
    grp = [m for m in T.tables["GRP"] if rank in m][0]
    peers = [T.cores[r] for r in grp if r != rank]

    def near(d):
        a, b = topo.chip(core), topo.chip(d)
        if a == b:
            return 2
        return 1 if (topo.mates(a, b) or topo.same_plane(a, b)) else 0
    peers.sort(key=near)
    mask = topo.mask(core, peers[0])
    for d in peers:
        mask &= topo.mask(core, d)
    return grp, peers, mask


def rank_program(g, core, T, topo):
    rank = T.rank_of(core)
    if rank is None:
        return
    grp, peers, mask = _peers(T, topo, core)
    R = len(grp)
    D = 128 * R
    c0 = 4 * grp.index(rank)
    S = T.sem
    A = ActivationFunctionType
    add, mult = AluOpType.add, AluOpType.mult
    V, SC, PE, SY = g.vector, g.scalar, g.tensor, g.sync
    xt = [T.xt0, T.xt1]
    xr = [T.xr0, T.xr1]
    yt = [T.yt0, T.yt1]

    def col(t, c):
        return t[:, c:c + 1]

    SY.dma_start(T.xs[:, 0:128], T.x[:, 0:128]).then_inc(S.ld0, 16)
    SC.dma_start(T.xs[:, 128:256], T.x[:, 128:256]).then_inc(S.ld1, 16)
    V.memset(T.negc[:], -1.0 / 128.0).then_inc(S.ng, 1)
    V.memset(T.ident[:], 1.0).then_inc(S.ones, 1)
    g.wait_ge(S.ones, 1)
    g.affine_select(T.ident[:], T.ident[:], [[-1, 128]], AluOpType.is_equal, 0.0, 0, 1).then_inc(S.idn, 1)

    PE.wait_ge(S.ng, 1)
    PE.wait_ge(S.ld0, 16)
    PE.matmul(T.pm[:, 0:1], T.xs[:, 0:128], T.negc[:, 0:1], True, True).then_inc(S.mm, 1)
    PE.wait_ge(S.idn, 1)
    PE.transpose(T.xt0[:, 0:128], T.xs[:, 0:128], T.ident[:]).then_inc(S.tp0, 1)
    PE.wait_ge(S.ld1, 16)
    PE.transpose(T.xt1[:, 0:128], T.xs[:, 128:256], T.ident[:]).then_inc(S.tp1, 1)
    V.wait_ge(S.mm, 1)
    V.tensor_copy(T.mh[:, 0:1], T.pm[:, 0:1]).then_inc(S.me, 1)
    V.tensor_copy(col(T.land, c0), T.pm[:, 0:1]).then_inc(S.ml, 1)
    SC.wait_ge(S.tp0, 1)
    SC.wait_ge(S.me, 1)
    SC.activation(T.ja[:], T.xt0[:, 0:128], A.Square, bias=T.mh[:, 0:1], scale=1.0,
                  accum_out=col(T.land, c0 + 2)).then_inc(S.sq0, 1)
    SC.wait_ge(S.tp1, 1)
    SC.activation(T.jb[:], T.xt1[:, 0:128], A.Copy, scale=-1.0 / 128.0,
                  accum_out=col(T.land, c0 + 1)).then_inc(S.mn1, 1)
    SC.wait_ge(S.mn1, 1)
    SC.activation(T.jc[:], T.xt1[:, 0:128], A.Square, bias=col(T.land, c0 + 1), scale=1.0,
                  accum_out=col(T.land, c0 + 3)).then_inc(S.sq1, 1)

    def ident_of(d):
        rid, pid, _se = topo.addr(d)
        return DstId(rid=rid, pnc=pid)

    near, far = peers[-1], peers[:-1]
    g.wait_ge(S.me, 1)
    g.remote_dma_fused([RemoteDMATransfer(dst_ids=[ident_of(near)], dma_engine_mask=mask, remote_sem=S.arr,
                                          srcs=[T.mh[:, 0:1]], dsts=[col(T.land, c0)], alu_op=0)], local_sem=S.sent)
    for n in ("ml", "mn1", "sq0", "sq1"):
        g.wait_ge(S[n], 1)
    slot = T.land[:, c0:c0 + 4]
    g.remote_dma_fused([RemoteDMATransfer(dst_ids=[ident_of(d) for d in far], dma_engine_mask=mask, remote_sem=S.arr,
                                          srcs=[slot], dsts=[slot for _d in far], alu_op=0)], local_sem=S.sent)
    rest = T.land[:, c0 + 1:c0 + 4]
    g.remote_dma_fused([RemoteDMATransfer(dst_ids=[ident_of(near)], dma_engine_mask=mask, remote_sem=S.arr,
                                          srcs=[rest], dsts=[rest], alu_op=0)], local_sem=S.sent)
    expect = 0
    for d in peers:
        _g, dp, dm = _peers(T, topo, d)
        expect += _bits(dm) * (2 if dp[-1] == core else 1)

    SC.wait_ge(S.sq0, 1)
    SC.wait_ge(S.sq1, 1)
    SC.activation(T.st[:, 14:16], T.land[:, c0 + 2:c0 + 4], A.Sqrt, bias=EPS, scale=1.0 / 128.0).then_inc(S.ow, 1)
    for n in ("tp0", "tp1", "sq0", "sq1", "ow"):
        V.wait_ge(S[n], 1)
    V.reciprocal(T.st[:, 16:18], T.st[:, 14:16]).then_inc(S.rw, 1)
    V.wait_ge(S.rw, 1)
    V.tensor_tensor(T.st[:, 18:20], T.st[:, 16:18], T.st[:, 16:18], mult).then_inc(S.rr, 1)
    for h in (0, 1):
        V.tensor_scalar(xr[h][:], xt[h][:, 0:128], col(T.st, 16 + h), None, mult).then_inc(S["xs%d" % h], 1)
    V.wait_ge(S.rr, 1)
    V.tensor_scalar(T.st[:, 20:22], T.st[:, 18:20], 1.0 / float(D), None, mult).then_inc(S.ra, 1)
    V.tensor_scalar(T.st[:, 22:24], T.st[:, 18:20], 1.0 / float(R ** 3), None, mult).then_inc(S.rb, 1)
    V.wait_ge(S.ra, 1)
    SC.wait_ge(S.rb, 1)

    SC.wait_ge(S.ml, 1)
    SC.wait_ge(S.arr, expect)
    for h in (0, 1):
        means = T.land[:, h:4 * R:4]
        SC.activation(T.jr[:, 16 * h:16 * h + R], means, A.Copy, scale=1.0,
                      accum_out=col(T.st, h)).then_inc(S["sm%d" % h], 1)
        SC.wait_ge(S["sm%d" % h], 1)
        SC.activation(T.jr[:, 16 * h + 8:16 * h + 8 + R], means, A.Square, bias=col(T.st, h), scale=-float(R),
                      accum_out=col(T.st, 2 + h)).then_inc(S["dv%d" % h], 1)
        SC.wait_ge(S["dv%d" % h], 1)
        SC.wait_ge(S["bb%d" % h], 1)
        SC.activation(col(T.st, 8 + h), col(T.st, 2 + h), A.Sqrt, bias=col(T.st, 6 + h),
                      scale=col(T.st, 22 + h)).then_inc(S["sd%d" % h], 1)
    V.wait_ge(S.arr, expect)
    for h in (0, 1):
        V.tensor_reduce(col(T.st, 4 + h), T.land[:, 2 + h:4 * R:4], AxisListType.X, add).then_inc(S["qq%d" % h], 1)
        V.wait_ge(S["qq%d" % h], 1)
        V.tensor_scalar(col(T.st, 6 + h), col(T.st, 4 + h), float(D) * EPS, col(T.st, 20 + h), add, mult).then_inc(
            S["bb%d" % h], 1)
    for h in (0, 1):
        V.wait_ge(S["sm%d" % h], 1)
        V.tensor_scalar(col(T.st, 12 + h), col(T.st, h), 1.0 / float(R), col(T.st, 16 + h), mult, mult).then_inc(
            S["nm%d" % h], 1)
        V.wait_ge(S["sd%d" % h], 1)
        V.reciprocal(col(T.st, 10 + h), col(T.st, 8 + h)).then_inc(S["rc%d" % h], 1)
        V.wait_ge(S["nm%d" % h], 1)
        V.wait_ge(S["rc%d" % h], 1)
        V.wait_ge(S["xs%d" % h], 1)
        V.tensor_scalar(yt[h][:], xr[h][:], col(T.st, 12 + h), col(T.st, 10 + h), add, mult).then_inc(
            S["nr%d" % h], 1)
    PE.wait_ge(S.nr0, 1)
    PE.transpose(T.yo0[:, 0:128], T.yt0[:], T.ident[:]).then_inc(S.tb0, 1)
    PE.wait_ge(S.nr1, 1)
    PE.transpose(T.yo1[:, 0:64], T.yt1[0:64, :], T.ident[0:64, 0:64]).then_inc(S.tb1, 1)
    PE.transpose(T.yo2[:, 0:64], T.yt1[64:128, :], T.ident[64:128, 64:128]).then_inc(S.tb2, 1)
    V.wait_ge(S.tb0, 1)
    V.tensor_copy(T.ys[:, 0:128], T.yo0[:, 0:128]).then_inc(S.cp0, 1)
    V.wait_ge(S.tb1, 1)
    V.tensor_copy(T.ys[:, 128:192], T.yo1[:, 0:64]).then_inc(S.cp1, 1)
    SC.wait_ge(S.tb2, 1)
    SC.activation(T.ys[:, 192:256], T.yo2[:, 0:64], A.Copy).then_inc(S.cp2, 1)
    SY.wait_ge(S.cp0, 1)
    SY.dma_start(T.y[:, 0:128], T.ys[:, 0:128]).then_inc(S.so0, 16)
    SY.wait_ge(S.cp1, 1)
    SY.dma_start(T.y[:, 128:192], T.ys[:, 128:192]).then_inc(S.so1, 16)
    SY.wait_ge(S.cp2, 1)
    SY.dma_start(T.y[:, 192:256], T.ys[:, 192:256]).then_inc(S.so2, 16)
    SY.wait_ge(S.so0, 16)
    SY.wait_ge(S.so1, 16)
    SY.wait_ge(S.so2, 16)
    g.wait_ge(S.sent, 3 * _bits(mask))
